import numpy as np, ml_dtypes
CORES = [49,52,55,57,60,63,65,68,71,73,76,79]
N = 12
GR, GC, TK = 3, 4, 256
RA = [[1,2,-1],[1,-2,-2],[1,-2,-2]]
CB = [[1,-1,2,1],[2,2,-2,-1],[-2,-1,-2,1],[1,1,-2,2]]
def setup_inputs(rng):
    return {"x": rng.standard_normal((N, 128, TK), dtype=np.float32).astype(ml_dtypes.bfloat16), "a": (rng.standard_normal((N, 128, 128), dtype=np.float32) / 11).astype(ml_dtypes.bfloat16)}
def setup_inputs_big(rng):
    d = setup_inputs(rng)
    for k in ("x", "a"): d[k] = (d[k].astype(np.float32) * 1024.0).astype(d[k].dtype)
    return d
def setup_inputs_small(rng):
    d = setup_inputs(rng)
    for k in ("x", "a"): d[k] = (d[k].astype(np.float32) * (1 / 1024.0)).astype(d[k].dtype)
    return d
def setup_inputs_apart(rng):
    d = setup_inputs(rng)
    f = (10.0 ** rng.permutation(np.linspace(-1.5, 1.5, N))).astype(np.float32).reshape(N, 1, 1)
    for k in ("x", "a"): d[k] = (d[k].astype(np.float32) * f).astype(d[k].dtype)
    return d
def reference(x, a):
    X, A = x.astype(np.float64), a.astype(np.float64)
    y = np.zeros((N, 128, TK))
    for i in range(GR):
        for j in range(GC):
            t = sum(RA[i][k] * CB[j][l] * X[k * GC + l] for k in range(GR) for l in range(GC))
            y[i * GC + j] = A[i * GC + j].T @ t
    return {"y": y.astype(ml_dtypes.bfloat16)}

@@ -1,0 +1,152 @@
+from concourse.bass import DstId, RemoteDMATransfer
+
+P = 128
+TK = 256
+NCOEF = 6
+NSLOT = 6
+
+SCRATCH = {
+    "raw": ("sbuf", [P, NSLOT * TK], "bfloat16"),
+    "a_sb": ("sbuf", [P, P], "bfloat16"),
+    "zb": ("sbuf", [P, NCOEF * P + 1], "bfloat16"),
+    "skew": ("dram", [1, P * (NCOEF * P + 1)], "bfloat16"),
+    "ident": ("sbuf", [P, NCOEF * P], "bfloat16"),
+    "pout": ("sbuf", [P, 4 * TK], "bfloat16"),
+    "pin": ("sbuf", [P, 2 * TK], "bfloat16"),
+    "y_sb": ("sbuf", [P, TK], "bfloat16"),
+    "ps0": ("psum", [P, 512], "float32"),
+    "ps1": ("psum", [P, 512], "float32"),
+    "ps2": ("psum", [P, 512], "float32"),
+    "ps3": ("psum", [P, 512], "float32"),
+    "psy": ("psum", [P, 512], "float32"),
+}
+SEMAPHORES = (["ldx", "lda", "fill", "sk1", "sk2", "sent", "pp", "pm", "mmy", "cpy", "st"]
+              + ["r%d" % k for k in range(NSLOT)] + ["mm%d" % k for k in range(4)] + ["cp%d" % k for k in range(4)])
+
+
+def _count(mask):
+    return bin(mask).count("1")
+
+
+def _layout(T, topo):
+    chips = sorted({topo.chip(c) for c in T.cores})
+    members = {ch: [c for c in T.cores if topo.chip(c) == ch] for ch in chips}
+    plane = {ch: [o for o in chips if topo.same_plane(ch, o)][0] for ch in chips}
+    mate = {ch: [o for o in chips if topo.mates(ch, o)][0] for ch in chips}
+    hub = {ch: [c for c in members[ch] if all(topo.may_write(c, d) for d in members[mate[ch]])][0] for ch in chips}
+    return members, plane, mate, hub
+
+
+def rank_program(g, core, T, topo):
+    rank = T.rank_of(core)
+    if rank is None:
+        return
+    RA, CB = T.tables["RA"], T.tables["CB"]
+    gc = len(CB)
+
+    def coef(dst_core, src_core):
+        d, s = T.rank_of(dst_core), T.rank_of(src_core)
+        return RA[d // gc][s // gc] * CB[d % gc][s % gc]
+
+    members, plane, mate, hub = _layout(T, topo)
+    ch = topo.chip(core)
+    mine, theirs = members[ch], members[plane[ch]]
+    is_hub = core == hub[ch]
+    idx = mine.index(core)
+    others = [c for c in mine if c != core]
+
+    def slot(k):
+        return T.raw[:, k * TK:(k + 1) * TK]
+
+    def dst_id(c):
+        rid, pid, _ = topo.addr(c)
+        return DstId(rid=rid, pnc=pid)
+
+    def by_die(cs):
+        return sorted(cs, key=lambda c: (topo.die(c), c))
+
+    if is_hub:
+        sources = [core] + others + theirs
+        n_tilewise = len(mine)
+        sends = [(d, 1, T.sem.pm) for d in members[mate[ch]]]
+    else:
+        sources = [core] + others
+        n_tilewise = 0
+        free_here = by_die([c for c in mine if c != hub[ch]])
+        free_there = by_die([c for c in theirs if c != hub[plane[ch]]])
+        sends = [(free_there[free_here.index(core)], 0, T.sem.pp)]
+    jobs = [d for d, _, _ in sends] + [core]
+    src_slot = {c: (mine.index(c) if c in mine else len(mine) + theirs.index(c)) for c in sources}
+    coefs = sorted({coef(d, s) for d in jobs for s in sources if coef(d, s) != 0}, key=lambda c: (abs(c), -c))
+    nc = len(coefs)
+
+    off = topo.mask(core, hub[plane[ch]])
+    on = topo.mask(core, others[0]) & ~off
+    n_off, n_on = _count(off), _count(on)
+
+    g.sync.dma_start(slot(idx), T.x[:]).then_inc(T.sem.ldx, 16)
+    g.scalar.dma_start(T.a_sb[:], T.a[:]).then_inc(T.sem.lda, 16)
+    for s, c in enumerate(coefs):
+        end = (s + 1) * P + (1 if s == nc - 1 else 0)
+        g.vector.memset(T.zb[:, s * P:s * P + 1], float(c)).then_inc(T.sem.fill, 1)
+        g.vector.memset(T.zb[:, s * P + 1:end], 0.0).then_inc(T.sem.fill, 1)
+    g.scalar.wait_ge(T.sem.fill, 2 * nc)
+    g.scalar.dma_start(T.skew[0, 0:P * (nc * P + 1)], T.zb[:, 0:nc * P + 1]).then_inc(T.sem.sk1, 16)
+    g.scalar.wait_ge(T.sem.sk1, 16)
+    g.scalar.dma_start(T.ident[:, 0:nc * P], T.skew[0, 0:P * nc * P]).then_inc(T.sem.sk2, 16)
+
+    first = sorted(others, key=lambda c: c != hub[ch])
+    g.wait_ge(T.sem.ldx, 16)
+    g.remote_dma_fused([
+        RemoteDMATransfer(dst_ids=[dst_id(hub[plane[ch]])], dma_engine_mask=off,
+                          remote_sem=T.sem["r%d" % (len(theirs) + idx)], src=slot(idx), dst=slot(len(theirs) + idx)),
+        RemoteDMATransfer(dst_ids=[dst_id(c) for c in first], dma_engine_mask=on,
+                          remote_sem=T.sem["r%d" % idx], srcs=[slot(idx)], dsts=[slot(idx) for _ in first]),
+    ], local_sem=T.sem.sent)
+    n_sent = n_off + n_on
+
+    out_jobs = list(range(len(sends)))
+    order = [(j, s) for s in sources[:n_tilewise] for j in out_jobs]
+    order += [(j, s) for j in out_jobs for s in sources[n_tilewise:]]
+    order += [(len(sends), s) for s in sources]
+    order = [(j, s) for j, s in order if coef(jobs[j], s) != 0]
+    g.tensor.wait_ge(T.sem.sk2, 16)
+    g.tensor.wait_ge(T.sem.ldx, 16)
+    here = {core}
+    begun = set()
+    for n, (j, s) in enumerate(order):
+        if s not in here:
+            here.add(s)
+            g.tensor.wait_ge(T.sem["r%d" % src_slot[s]], n_on if s in mine else n_off)
+        last = all(j2 != j for j2, _ in order[n + 1:])
+        k = coefs.index(coef(jobs[j], s))
+        mm = g.tensor.matmul(T["ps%d" % j][:, 0:TK], T.ident[:, k * P:(k + 1) * P], slot(src_slot[s]), j not in begun, last)
+        begun.add(j)
+        if last:
+            mm.then_inc(T.sem["mm%d" % j], 1)
+
+    for j in range(len(jobs)):
+        g.vector.wait_ge(T.sem["mm%d" % j], 1)
+        g.vector.tensor_copy(T.pout[:, j * TK:(j + 1) * TK], T["ps%d" % j][:, 0:TK]).then_inc(T.sem["cp%d" % j], 1)
+    for j, (d, land, sem) in enumerate(sends):
+        rid, pid, _ = topo.addr(d)
+        m = topo.mask(core, d)
+        g.wait_ge(T.sem["cp%d" % j], 1)
+        g.remote_dma(T.pin[:, land * TK:(land + 1) * TK], T.pout[:, j * TK:(j + 1) * TK], sem, T.sem.sent, pid, rid, m)
+        n_sent += _count(m)
+
+    own = len(sends)
+    g.tensor.wait_ge(T.sem.lda, 16)
+    g.tensor.wait_ge(T.sem["cp%d" % own], 1)
+    g.tensor.matmul(T.psy[:, 0:TK], T.a_sb[:], T.pout[:, own * TK:(own + 1) * TK], True, False)
+    if not is_hub:
+        g.tensor.wait_ge(T.sem.pp, n_off)
+        g.tensor.matmul(T.psy[:, 0:TK], T.a_sb[:], T.pin[:, 0:TK], False, False)
+    g.tensor.wait_ge(T.sem.pm, n_off)
+    g.tensor.matmul(T.psy[:, 0:TK], T.a_sb[:], T.pin[:, TK:2 * TK], False, True).then_inc(T.sem.mmy, 1)
+    g.vector.wait_ge(T.sem.mmy, 1)
+    g.vector.tensor_copy(T.y_sb[:], T.psy[:, 0:TK]).then_inc(T.sem.cpy, 1)
+    g.sync.wait_ge(T.sem.cpy, 1)
+    g.sync.dma_start(T.y[:], T.y_sb[:]).then_inc(T.sem.st, 16)
+    g.sync.wait_ge(T.sem.st, 16)
+    g.wait_ge(T.sem.sent, n_sent)

@@ -1,27 +1,30 @@
 from concourse.bass import DstId, RemoteDMATransfer
+from concourse.mybir import AluOpType, ActivationFunctionType
 
 P = 128
 TK = 256
-NCOEF = 6
+H = TK // 2
 NSLOT = 6
+NID = 10
+NA = 6
 
 SCRATCH = {
     "raw": ("sbuf", [P, NSLOT * TK], "bfloat16"),
     "a_sb": ("sbuf", [P, P], "bfloat16"),
-    "zb": ("sbuf", [P, NCOEF * P + 1], "bfloat16"),
-    "skew": ("dram", [1, P * (NCOEF * P + 1)], "bfloat16"),
-    "ident": ("sbuf", [P, NCOEF * P], "bfloat16"),
-    "pout": ("sbuf", [P, 4 * TK], "bfloat16"),
+    "a_sc": ("sbuf", [P, NA * P], "bfloat16"),
+    "id1": ("sbuf", [P, P], "bfloat16"),
+    "ident": ("sbuf", [P, NID * P], "bfloat16"),
+    "pout": ("sbuf", [P, 3 * TK], "bfloat16"),
     "pin": ("sbuf", [P, 2 * TK], "bfloat16"),
     "y_sb": ("sbuf", [P, TK], "bfloat16"),
     "ps0": ("psum", [P, 512], "float32"),
     "ps1": ("psum", [P, 512], "float32"),
     "ps2": ("psum", [P, 512], "float32"),
-    "ps3": ("psum", [P, 512], "float32"),
-    "psy": ("psum", [P, 512], "float32"),
+    "psy0": ("psum", [P, 512], "float32"),
+    "psy1": ("psum", [P, 512], "float32"),
 }
-SEMAPHORES = (["ldx", "lda", "fill", "sk1", "sk2", "sent", "pp", "pm", "mmy", "cpy", "st"]
-              + ["r%d" % k for k in range(NSLOT)] + ["mm%d" % k for k in range(4)] + ["cp%d" % k for k in range(4)])
+SEMAPHORES = (["ldx", "lda", "fill", "sel", "idn", "sa", "sent1", "sent", "pp", "pm", "my0", "my1", "cpy", "st"]
+              + ["r%d" % k for k in range(NSLOT)] + ["mm%d" % k for k in range(3)] + ["cp%d" % k for k in range(3)])
 
 
 def _count(mask):
@@ -55,6 +58,17 @@ def rank_program(g, core, T, topo):
     idx = mine.index(core)
     others = [c for c in mine if c != core]
 
+    def held(c):
+        cc = topo.chip(c)
+        own_chip = [c] + [o for o in members[cc] if o != c]
+        return own_chip + members[plane[cc]] if c == hub[cc] else own_chip
+
+    def norm(dst_core, sender):
+        return coef(dst_core, held(sender)[-1])
+
+    def free(cc):
+        return sorted([c for c in members[cc] if c != hub[cc]], key=lambda c: (topo.die(c), c))
+
     def slot(k):
         return T.raw[:, k * TK:(k + 1) * TK]
 
@@ -62,38 +76,54 @@ def rank_program(g, core, T, topo):
         rid, pid, _ = topo.addr(c)
         return DstId(rid=rid, pnc=pid)
 
-    def by_die(cs):
-        return sorted(cs, key=lambda c: (topo.die(c), c))
-
+    sources = held(core)
     if is_hub:
-        sources = [core] + others + theirs
         n_tilewise = len(mine)
         sends = [(d, 1, T.sem.pm) for d in members[mate[ch]]]
+        switch_sender = None
     else:
-        sources = [core] + others
         n_tilewise = 0
-        free_here = by_die([c for c in mine if c != hub[ch]])
-        free_there = by_die([c for c in theirs if c != hub[plane[ch]]])
-        sends = [(free_there[free_here.index(core)], 0, T.sem.pp)]
-    jobs = [d for d, _, _ in sends] + [core]
+        switch_sender = free(plane[ch])[free(ch).index(core)]
+        sends = [(switch_sender, 0, T.sem.pp)]
     src_slot = {c: (mine.index(c) if c in mine else len(mine) + theirs.index(c)) for c in sources}
-    coefs = sorted({coef(d, s) for d in jobs for s in sources if coef(d, s) != 0}, key=lambda c: (abs(c), -c))
-    nc = len(coefs)
+    last_src = sources[-1]
+
+    def quot(d, s):
+        return coef(d, s) / norm(d, core)
+
+    quots = sorted({quot(d, s) for d, _, _ in sends for s in sources[:-1]} - {1.0})
+    a_need = {coef(core, s) for s in sources} | {norm(core, hub[mate[ch]])}
+    if switch_sender is not None:
+        a_need.add(norm(core, switch_sender))
+    a_coefs = sorted(a_need - {1})
+
+    def ident(q):
+        if q == 1.0:
+            return T.id1[:]
+        k = quots.index(q)
+        return T.ident[:, k * P:(k + 1) * P]
+
+    def a_times(c):
+        if c == 1:
+            return T.a_sb[:]
+        k = a_coefs.index(c)
+        return T.a_sc[:, k * P:(k + 1) * P]
 
     off = topo.mask(core, hub[plane[ch]])
     on = topo.mask(core, others[0]) & ~off
     n_off, n_on = _count(off), _count(on)
 
+    def arrival(s):
+        return T.sem["r%d" % src_slot[s]], (n_on if s in mine else n_off)
+
     g.sync.dma_start(slot(idx), T.x[:]).then_inc(T.sem.ldx, 16)
-    g.scalar.dma_start(T.a_sb[:], T.a[:]).then_inc(T.sem.lda, 16)
-    for s, c in enumerate(coefs):
-        end = (s + 1) * P + (1 if s == nc - 1 else 0)
-        g.vector.memset(T.zb[:, s * P:s * P + 1], float(c)).then_inc(T.sem.fill, 1)
-        g.vector.memset(T.zb[:, s * P + 1:end], 0.0).then_inc(T.sem.fill, 1)
-    g.scalar.wait_ge(T.sem.fill, 2 * nc)
-    g.scalar.dma_start(T.skew[0, 0:P * (nc * P + 1)], T.zb[:, 0:nc * P + 1]).then_inc(T.sem.sk1, 16)
-    g.scalar.wait_ge(T.sem.sk1, 16)
-    g.scalar.dma_start(T.ident[:, 0:nc * P], T.skew[0, 0:P * nc * P]).then_inc(T.sem.sk2, 16)
+
+    g.vector.memset(T.id1[:], 1.0).then_inc(T.sem.fill, 1)
+    g.wait_ge(T.sem.fill, 1)
+    g.affine_select(T.id1[:], T.id1[:], [[-1, P]], AluOpType.is_equal, 0.0, 0, 1).then_inc(T.sem.sel, 1)
+    g.vector.wait_ge(T.sem.sel, 1)
+    for k, q in enumerate(quots):
+        g.vector.tensor_scalar(T.ident[:, k * P:(k + 1) * P], T.id1[:], float(q), None, AluOpType.mult).then_inc(T.sem.idn, 1)
 
     first = sorted(others, key=lambda c: c != hub[ch])
     g.wait_ge(T.sem.ldx, 16)
@@ -102,32 +132,41 @@ def rank_program(g, core, T, topo):
                           remote_sem=T.sem["r%d" % (len(theirs) + idx)], src=slot(idx), dst=slot(len(theirs) + idx)),
         RemoteDMATransfer(dst_ids=[dst_id(c) for c in first], dma_engine_mask=on,
                           remote_sem=T.sem["r%d" % idx], srcs=[slot(idx)], dsts=[slot(idx) for _ in first]),
-    ], local_sem=T.sem.sent)
-    n_sent = n_off + n_on
+    ], local_sem=T.sem.sent1)
 
-    out_jobs = list(range(len(sends)))
-    order = [(j, s) for s in sources[:n_tilewise] for j in out_jobs]
-    order += [(j, s) for j in out_jobs for s in sources[n_tilewise:]]
-    order += [(len(sends), s) for s in sources]
-    order = [(j, s) for j, s in order if coef(jobs[j], s) != 0]
-    g.tensor.wait_ge(T.sem.sk2, 16)
+    g.scalar.wait_ge(T.sem.sent1, n_off + n_on)
+    g.scalar.dma_start(T.a_sb[:], T.a[:]).then_inc(T.sem.lda, 16)
+    g.scalar.wait_ge(T.sem.lda, 16)
+    for k, c in enumerate(a_coefs):
+        g.scalar.activation(T.a_sc[:, k * P:(k + 1) * P], T.a_sb[:], ActivationFunctionType.Copy,
+                            scale=float(c)).then_inc(T.sem.sa, 1)
+
+    jobs = list(range(len(sends)))
+    by_pe = sources[:-1]
+    order = [(j, s) for s in by_pe[:n_tilewise] for j in jobs]
+    order += [(j, s) for j in jobs for s in by_pe[n_tilewise:]]
+    g.tensor.wait_ge(T.sem.sel, 1)
+    if quots:
+        g.tensor.wait_ge(T.sem.idn, len(quots))
     g.tensor.wait_ge(T.sem.ldx, 16)
     here = {core}
     begun = set()
     for n, (j, s) in enumerate(order):
         if s not in here:
             here.add(s)
-            g.tensor.wait_ge(T.sem["r%d" % src_slot[s]], n_on if s in mine else n_off)
+            g.tensor.wait_ge(*arrival(s))
         last = all(j2 != j for j2, _ in order[n + 1:])
-        k = coefs.index(coef(jobs[j], s))
-        mm = g.tensor.matmul(T["ps%d" % j][:, 0:TK], T.ident[:, k * P:(k + 1) * P], slot(src_slot[s]), j not in begun, last)
+        mm = g.tensor.matmul(T["ps%d" % j][:, 0:TK], ident(quot(sends[j][0], s)), slot(src_slot[s]), j not in begun, last)
         begun.add(j)
         if last:
             mm.then_inc(T.sem["mm%d" % j], 1)
 
-    for j in range(len(jobs)):
+    g.vector.wait_ge(*arrival(last_src))
+    for j in jobs:
         g.vector.wait_ge(T.sem["mm%d" % j], 1)
-        g.vector.tensor_copy(T.pout[:, j * TK:(j + 1) * TK], T["ps%d" % j][:, 0:TK]).then_inc(T.sem["cp%d" % j], 1)
+        g.vector.tensor_tensor(T.pout[:, j * TK:(j + 1) * TK], T["ps%d" % j][:, 0:TK], slot(src_slot[last_src]),
+                               AluOpType.add).then_inc(T.sem["cp%d" % j], 1)
+    n_sent = 0
     for j, (d, land, sem) in enumerate(sends):
         rid, pid, _ = topo.addr(d)
         m = topo.mask(core, d)
@@ -135,18 +174,31 @@ def rank_program(g, core, T, topo):
         g.remote_dma(T.pin[:, land * TK:(land + 1) * TK], T.pout[:, j * TK:(j + 1) * TK], sem, T.sem.sent, pid, rid, m)
         n_sent += _count(m)
 
-    own = len(sends)
+    halves = (0, 1)
     g.tensor.wait_ge(T.sem.lda, 16)
-    g.tensor.wait_ge(T.sem["cp%d" % own], 1)
-    g.tensor.matmul(T.psy[:, 0:TK], T.a_sb[:], T.pout[:, own * TK:(own + 1) * TK], True, False)
-    if not is_hub:
+    if a_coefs:
+        g.tensor.wait_ge(T.sem.sa, len(a_coefs))
+    for n, s in enumerate(sources):
+        if s not in here:
+            here.add(s)
+            g.tensor.wait_ge(*arrival(s))
+        k = src_slot[s]
+        for h in halves:
+            g.tensor.matmul(T["psy%d" % h][:, 0:H], a_times(coef(core, s)),
+                            T.raw[:, k * TK + h * H:k * TK + (h + 1) * H], n == 0, False)
+    if switch_sender is not None:
         g.tensor.wait_ge(T.sem.pp, n_off)
-        g.tensor.matmul(T.psy[:, 0:TK], T.a_sb[:], T.pin[:, 0:TK], False, False)
+        for h in halves:
+            g.tensor.matmul(T["psy%d" % h][:, 0:H], a_times(norm(core, switch_sender)),
+                            T.pin[:, h * H:(h + 1) * H], False, False)
     g.tensor.wait_ge(T.sem.pm, n_off)
-    g.tensor.matmul(T.psy[:, 0:TK], T.a_sb[:], T.pin[:, TK:2 * TK], False, True).then_inc(T.sem.mmy, 1)
-    g.vector.wait_ge(T.sem.mmy, 1)
-    g.vector.tensor_copy(T.y_sb[:], T.psy[:, 0:TK]).then_inc(T.sem.cpy, 1)
-    g.sync.wait_ge(T.sem.cpy, 1)
+    for h in halves:
+        g.tensor.matmul(T["psy%d" % h][:, 0:H], a_times(norm(core, hub[mate[ch]])),
+                        T.pin[:, TK + h * H:TK + (h + 1) * H], False, True).then_inc(T.sem["my%d" % h], 1)
+    for h in halves:
+        g.vector.wait_ge(T.sem["my%d" % h], 1)
+        g.vector.tensor_copy(T.y_sb[:, h * H:(h + 1) * H], T["psy%d" % h][:, 0:H]).then_inc(T.sem.cpy, 1)
+    g.sync.wait_ge(T.sem.cpy, len(halves))
     g.sync.dma_start(T.y[:], T.y_sb[:]).then_inc(T.sem.st, 16)
     g.sync.wait_ge(T.sem.st, 16)
     g.wait_ge(T.sem.sent, n_sent)

from concourse.bass import DstId, RemoteDMATransfer
from concourse.mybir import AluOpType, ActivationFunctionType

P = 128
TK = 256
H = TK // 2
NSLOT = 6
NID = 10
NA = 6

SCRATCH = {
    "raw": ("sbuf", [P, NSLOT * TK], "bfloat16"),
    "a_sb": ("sbuf", [P, P], "bfloat16"),
    "a_sc": ("sbuf", [P, NA * P], "bfloat16"),
    "id1": ("sbuf", [P, P], "bfloat16"),
    "ident": ("sbuf", [P, NID * P], "bfloat16"),
    "pout": ("sbuf", [P, 3 * TK], "bfloat16"),
    "pin": ("sbuf", [P, 2 * TK], "bfloat16"),
    "y_sb": ("sbuf", [P, TK], "bfloat16"),
    "ps0": ("psum", [P, 512], "float32"),
    "ps1": ("psum", [P, 512], "float32"),
    "ps2": ("psum", [P, 512], "float32"),
    "psy0": ("psum", [P, 512], "float32"),
    "psy1": ("psum", [P, 512], "float32"),
}
SEMAPHORES = (["ldx", "lda", "fill", "sel", "idn", "sa", "sent1", "sent", "pp", "pm", "my0", "my1", "cpy", "st"]
              + ["r%d" % k for k in range(NSLOT)] + ["mm%d" % k for k in range(3)] + ["cp%d" % k for k in range(3)])


def _count(mask):
    return bin(mask).count("1")


def _layout(T, topo):
    chips = sorted({topo.chip(c) for c in T.cores})
    members = {ch: [c for c in T.cores if topo.chip(c) == ch] for ch in chips}
    plane = {ch: [o for o in chips if topo.same_plane(ch, o)][0] for ch in chips}
    mate = {ch: [o for o in chips if topo.mates(ch, o)][0] for ch in chips}
    hub = {ch: [c for c in members[ch] if all(topo.may_write(c, d) for d in members[mate[ch]])][0] for ch in chips}
    return members, plane, mate, hub


def rank_program(g, core, T, topo):
    rank = T.rank_of(core)
    if rank is None:
        return
    RA, CB = T.tables["RA"], T.tables["CB"]
    gc = len(CB)

    def coef(dst_core, src_core):
        d, s = T.rank_of(dst_core), T.rank_of(src_core)
        return RA[d // gc][s // gc] * CB[d % gc][s % gc]

    members, plane, mate, hub = _layout(T, topo)
    ch = topo.chip(core)
    mine, theirs = members[ch], members[plane[ch]]
    is_hub = core == hub[ch]
    idx = mine.index(core)
    others = [c for c in mine if c != core]

    def held(c):
        cc = topo.chip(c)
        own_chip = [c] + [o for o in members[cc] if o != c]
        return own_chip + members[plane[cc]] if c == hub[cc] else own_chip

    def norm(dst_core, sender):
        return coef(dst_core, held(sender)[-1])

    def free(cc):
        return sorted([c for c in members[cc] if c != hub[cc]], key=lambda c: (topo.die(c), c))

    def slot(k):
        return T.raw[:, k * TK:(k + 1) * TK]

    def dst_id(c):
        rid, pid, _ = topo.addr(c)
        return DstId(rid=rid, pnc=pid)

    sources = held(core)
    if is_hub:
        n_tilewise = len(mine)
        sends = [(d, 1, T.sem.pm) for d in members[mate[ch]]]
        switch_sender = None
    else:
        n_tilewise = 0
        switch_sender = free(plane[ch])[free(ch).index(core)]
        sends = [(switch_sender, 0, T.sem.pp)]
    src_slot = {c: (mine.index(c) if c in mine else len(mine) + theirs.index(c)) for c in sources}
    last_src = sources[-1]

    def quot(d, s):
        return coef(d, s) / norm(d, core)

    quots = sorted({quot(d, s) for d, _, _ in sends for s in sources[:-1]} - {1.0})
    a_need = {coef(core, s) for s in sources} | {norm(core, hub[mate[ch]])}
    if switch_sender is not None:
        a_need.add(norm(core, switch_sender))
    a_coefs = sorted(a_need - {1})

    def ident(q):
        if q == 1.0:
            return T.id1[:]
        k = quots.index(q)
        return T.ident[:, k * P:(k + 1) * P]

    def a_times(c):
        if c == 1:
            return T.a_sb[:]
        k = a_coefs.index(c)
        return T.a_sc[:, k * P:(k + 1) * P]

    off = topo.mask(core, hub[plane[ch]])
    on = topo.mask(core, others[0]) & ~off
    n_off, n_on = _count(off), _count(on)

    def arrival(s):
        return T.sem["r%d" % src_slot[s]], (n_on if s in mine else n_off)

    g.sync.dma_start(slot(idx), T.x[:]).then_inc(T.sem.ldx, 16)

    g.vector.memset(T.id1[:], 1.0).then_inc(T.sem.fill, 1)
    g.wait_ge(T.sem.fill, 1)
    g.affine_select(T.id1[:], T.id1[:], [[-1, P]], AluOpType.is_equal, 0.0, 0, 1).then_inc(T.sem.sel, 1)
    g.vector.wait_ge(T.sem.sel, 1)
    for k, q in enumerate(quots):
        g.vector.tensor_scalar(T.ident[:, k * P:(k + 1) * P], T.id1[:], float(q), None, AluOpType.mult).then_inc(T.sem.idn, 1)

    first = sorted(others, key=lambda c: c != hub[ch])
    g.wait_ge(T.sem.ldx, 16)
    g.remote_dma_fused([
        RemoteDMATransfer(dst_ids=[dst_id(hub[plane[ch]])], dma_engine_mask=off,
                          remote_sem=T.sem["r%d" % (len(theirs) + idx)], src=slot(idx), dst=slot(len(theirs) + idx)),
        RemoteDMATransfer(dst_ids=[dst_id(c) for c in first], dma_engine_mask=on,
                          remote_sem=T.sem["r%d" % idx], srcs=[slot(idx)], dsts=[slot(idx) for _ in first]),
    ], local_sem=T.sem.sent1)

    g.scalar.wait_ge(T.sem.sent1, n_off + n_on)
    g.scalar.dma_start(T.a_sb[:], T.a[:]).then_inc(T.sem.lda, 16)
    g.scalar.wait_ge(T.sem.lda, 16)
    for k, c in enumerate(a_coefs):
        g.scalar.activation(T.a_sc[:, k * P:(k + 1) * P], T.a_sb[:], ActivationFunctionType.Copy,
                            scale=float(c)).then_inc(T.sem.sa, 1)

    jobs = list(range(len(sends)))
    by_pe = sources[:-1]
    order = [(j, s) for s in by_pe[:n_tilewise] for j in jobs]
    order += [(j, s) for j in jobs for s in by_pe[n_tilewise:]]
    g.tensor.wait_ge(T.sem.sel, 1)
    if quots:
        g.tensor.wait_ge(T.sem.idn, len(quots))
    g.tensor.wait_ge(T.sem.ldx, 16)
    here = {core}
    begun = set()
    for n, (j, s) in enumerate(order):
        if s not in here:
            here.add(s)
            g.tensor.wait_ge(*arrival(s))
        last = all(j2 != j for j2, _ in order[n + 1:])
        mm = g.tensor.matmul(T["ps%d" % j][:, 0:TK], ident(quot(sends[j][0], s)), slot(src_slot[s]), j not in begun, last)
        begun.add(j)
        if last:
            mm.then_inc(T.sem["mm%d" % j], 1)

    g.vector.wait_ge(*arrival(last_src))
    for j in jobs:
        g.vector.wait_ge(T.sem["mm%d" % j], 1)
        g.vector.tensor_tensor(T.pout[:, j * TK:(j + 1) * TK], T["ps%d" % j][:, 0:TK], slot(src_slot[last_src]),
                               AluOpType.add).then_inc(T.sem["cp%d" % j], 1)
    n_sent = 0
    for j, (d, land, sem) in enumerate(sends):
        rid, pid, _ = topo.addr(d)
        m = topo.mask(core, d)
        g.wait_ge(T.sem["cp%d" % j], 1)
        g.remote_dma(T.pin[:, land * TK:(land + 1) * TK], T.pout[:, j * TK:(j + 1) * TK], sem, T.sem.sent, pid, rid, m)
        n_sent += _count(m)

    halves = (0, 1)
    g.tensor.wait_ge(T.sem.lda, 16)
    if a_coefs:
        g.tensor.wait_ge(T.sem.sa, len(a_coefs))
    for n, s in enumerate(sources):
        if s not in here:
            here.add(s)
            g.tensor.wait_ge(*arrival(s))
        k = src_slot[s]
        for h in halves:
            g.tensor.matmul(T["psy%d" % h][:, 0:H], a_times(coef(core, s)),
                            T.raw[:, k * TK + h * H:k * TK + (h + 1) * H], n == 0, False)
    if switch_sender is not None:
        g.tensor.wait_ge(T.sem.pp, n_off)
        for h in halves:
            g.tensor.matmul(T["psy%d" % h][:, 0:H], a_times(norm(core, switch_sender)),
                            T.pin[:, h * H:(h + 1) * H], False, False)
    g.tensor.wait_ge(T.sem.pm, n_off)
    for h in halves:
        g.tensor.matmul(T["psy%d" % h][:, 0:H], a_times(norm(core, hub[mate[ch]])),
                        T.pin[:, TK + h * H:TK + (h + 1) * H], False, True).then_inc(T.sem["my%d" % h], 1)
    for h in halves:
        g.vector.wait_ge(T.sem["my%d" % h], 1)
        g.vector.tensor_copy(T.y_sb[:, h * H:(h + 1) * H], T["psy%d" % h][:, 0:H]).then_inc(T.sem.cpy, 1)
    g.sync.wait_ge(T.sem.cpy, len(halves))
    g.sync.dma_start(T.y[:], T.y_sb[:]).then_inc(T.sem.st, 16)
    g.sync.wait_ge(T.sem.st, 16)
    g.wait_ge(T.sem.sent, n_sent)
